import numpy as np
import ml_dtypes


def mxq(x, axis, fmt="e4m3"):
    dtype, down = {"e4m3": (ml_dtypes.float8_e4m3fn, 7), "e5m2": (ml_dtypes.float8_e5m2, 14)}[fmt]
    v = np.moveaxis(np.asarray(x, np.float32).astype(ml_dtypes.bfloat16).astype(np.float64), axis, -1)
    blocks = v.reshape(v.shape[:-1] + (-1, 32))
    amax = np.abs(blocks).max(-1, keepdims=True)
    byte = np.maximum(np.where(amax > 0, np.frexp(amax)[1] - 1 + 127, 0) - down, 1)
    scale = np.exp2(byte - 127.0)
    codes = (blocks / scale).astype(np.float32).astype(dtype).astype(np.float64)
    return np.moveaxis((codes * scale).reshape(v.shape), -1, axis)


WIDE = False


def mx_kscale(k):
    if not WIDE:
        return np.ones(k)
    levels = np.array([30, -30])
    if k % 512:
        return np.exp2(np.random.permutation(np.resize(levels, k // 32))).repeat(32)
    a = np.empty((k // 512, 16))
    for p in range(k // 512):
        a[p, :8] = np.random.permutation(np.resize(levels, 8))
        for g in range(8):
            far = levels[np.abs(levels - a[p, g]) >= 10]
            a[p, g + 8] = far[np.random.randint(len(far))]
    return np.exp2(a.ravel()).repeat(32)


BF16 = ml_dtypes.bfloat16


def bf(x):
    return np.asarray(x, np.float32).astype(BF16)


def f64(x):
    return np.asarray(x).astype(np.float64)


E2M1 = np.array([0.0, 0.5, 1.0, 1.5, 2.0, 3.0, 4.0, 6.0, -0.0, -0.5, -1.0, -1.5, -2.0, -3.0, -4.0, -6.0])


def pack_weight(w, fmt):
    k, n = w.shape
    w = f64(bf(w)).reshape(k // 32, 32, n)
    amax = np.abs(w).max(1)
    if fmt in ("e4m3", "e5m2"):
        byte = np.frexp(amax)[1] - 1 + 127 - (7 if fmt == "e4m3" else 14)
    else:
        mant, ex = np.frexp(amax / 6.0)
        byte = np.where(mant > 0.5, ex, ex - 1) + 127
    byte = np.clip(np.where(amax > 0, byte, 1), 1, 254)
    scaled = (w * np.exp2(127.0 - byte)[:, None, :]).reshape(k, n).astype(np.float32)
    by_word = np.ascontiguousarray(scaled.reshape(k // 512, 128, 4, n).transpose(0, 1, 3, 2))
    if fmt in ("e4m3", "e5m2"):
        words = by_word.astype(ml_dtypes.float8_e4m3fn if fmt == "e4m3" else ml_dtypes.float8_e5m2).view(np.uint8)
    else:
        c = by_word.astype(ml_dtypes.float4_e2m1fn).view(np.uint8) & 0xF
        words = c[..., 0::2] | (c[..., 1::2] << 4)
    return np.ascontiguousarray(words), np.ascontiguousarray(byte.astype(np.uint8).reshape(k // 512, 16, n))


def unpack_weight(words, scales, fmt):
    g, p, n, _ = words.shape
    if fmt in ("e4m3", "e5m2"):
        vals = np.ascontiguousarray(words).view(ml_dtypes.float8_e4m3fn if fmt == "e4m3" else ml_dtypes.float8_e5m2).astype(np.float64)
    else:
        nib = np.empty((g, p, n, 4), np.uint8)
        nib[..., 0::2] = words & 0xF
        nib[..., 1::2] = words >> 4
        vals = E2M1[nib]
    vals = vals * np.repeat(np.exp2(scales.astype(np.float64) - 127.0), 8, axis=1)[..., None]
    return vals.transpose(0, 1, 3, 2).reshape(g * 512, n)


F, S, I, B = 1536, 2048, 1024, 512


def setup_inputs():
    s, t = mx_kscale(F), mx_kscale(I)
    shocks = np.random.standard_t(5, (F, S)) * s[:, None]
    g_words, g_scales = pack_weight(shocks, "e5m2")
    delta = np.random.standard_normal((I, F)) / np.sqrt(F) / s * t[:, None]
    carry = 0.3 * np.random.standard_normal(I) * t
    stress = np.exp(0.4 * np.random.standard_normal((S, I)))
    hold = np.random.standard_normal((I, B)) / np.sqrt(I) / t[:, None]
    hedge = 0.5 * np.random.standard_normal((S, B))
    return {"g_words": g_words, "g_scales": g_scales,
            "delta": bf(delta), "carry": bf(carry), "stress": bf(stress),
            "hold": bf(hold), "hedge": bf(hedge)}


def reference(g_words, g_scales, delta, carry, stress, hold, hedge):
    g = unpack_weight(g_words, g_scales, "e5m2")
    d = mxq(f64(delta), 1, "e4m3")
    unit = g.T @ d.T
    pnl = (unit + f64(carry)) * f64(stress)
    h = mxq(f64(hold), 0, "e4m3")
    book = mxq(pnl, 1, "e5m2") @ h
    return book + f64(hedge)

@@ -1,0 +1,292 @@
+from contextlib import ExitStack
+
+import concourse.mybir as mybir
+from concourse.masks import make_identity
+
+F, S, I, B = 1536, 2048, 1024, 512
+FLOPS = 2 * S * F * I + 2 * S * I * B
+
+F32 = mybir.dt.float32
+BF16 = mybir.dt.bfloat16
+U32 = mybir.dt.uint32
+I32 = mybir.dt.int32
+U8 = mybir.dt.uint8
+E4 = mybir.dt.float8_e4m3fn_x4
+E5 = mybir.dt.float8_e5m2_x4
+ACT = mybir.ActivationFunctionType
+ALU = mybir.AluOpType
+
+P = 128
+A = F // 512
+G = I // 512
+SC = 512
+C = S // SC
+J = SC // P
+
+
+def tile_scenario_book_pnl_e3_kernel(tc, g_words, g_scales, delta, carry, stress, hold, hedge, out):
+    nc = tc.nc
+    with ExitStack() as ctx:
+        keep = ctx.enter_context(tc.tile_pool(name="keep", bufs=1))
+        work = ctx.enter_context(tc.tile_pool(name="work", bufs=3))
+        psum = ctx.enter_context(tc.psum_pool(name="psum", bufs=2))
+
+        ident = keep.tile([P, P], F32, name="ident")
+        make_identity(nc, ident[:])
+
+        d_raw = []
+        for i in range(8):
+            d_raw.append(keep.tile([P, F], BF16, name="d_raw%d" % i))
+        gw = []
+        st = []
+        hg = []
+        for c in range(C):
+            gw.append(keep.tile([P, A, SC], U32, name="gw%d" % c, align_bytes=64))
+            st.append(keep.tile([P, J, I], BF16, name="st%d" % c))
+            hg.append(keep.tile([P, J, B], BF16, name="hg%d" % c))
+        gs = keep.tile([P, A, S], U8, name="gs", align_bytes=64)
+        h_raw = keep.tile([P, G, 4, B], BF16, name="h_raw")
+        h_grp = keep.tile([P, G, B, 4], BF16, name="h_grp", align_bytes=64)
+        h_codes = keep.tile([P, G, B], U32, name="h_codes", align_bytes=64)
+        h_sc = keep.tile([P, G, B], U8, name="h_sc", align_bytes=64)
+        ca_raw = keep.tile([P, G, 4], BF16, name="ca_raw")
+        ca = keep.tile([P, G, 4], F32, name="ca")
+        d_codes = []
+        d_sc = []
+        for i in range(8):
+            d_codes.append(keep.tile([P, A, P], U32, name="d_codes%d" % i, align_bytes=64))
+            d_sc.append(keep.tile([P, A, P], U8, name="d_sc%d" % i, align_bytes=64))
+
+        d_view = delta.rearrange("(g m t) k -> g t m k", g=G, t=4)
+        gw_view = g_words.rearrange("g p n t -> p g (n t)")
+        gs_view = g_scales.bitcast(I32)
+        st_view = stress.rearrange("(c j p) i -> c p j i", c=C, p=P)
+        hg_view = hedge.rearrange("(c j p) b -> c p j b", c=C, p=P)
+
+        units = {}
+        stress_t = {}
+        pnl = {}
+        pnl_codes = {}
+        pnl_sc = {}
+        d_bank = {}
+        d_grp = {}
+
+        def load_d(i):
+            nc.sync.dma_start(out=d_raw[i][:], in_=d_view[i // 4, i % 4])
+
+        def load_g(c):
+            nc.sync.dma_start(out=gw[c][:].bitcast(I32), in_=gw_view[:, :, 2048 * c : 2048 * (c + 1)].bitcast(I32))
+
+        def load_st(c):
+            nc.sync.dma_start(out=st[c][:], in_=st_view[c])
+
+        def load_hg(c):
+            nc.sync.dma_start(out=hg[c][:], in_=hg_view[c])
+
+        def t_delta(i):
+            bank_a = psum.tile([P, 2, 2, P], F32, name="tr", bufs=4)
+            bank_b = psum.tile([P, 1, 2, P], F32, name="tr", bufs=4)
+            words = d_raw[i][:].bitcast(F32)
+            for a in range(A):
+                for u in range(2):
+                    dst = bank_a[:, a, u, :] if a < 2 else bank_b[:, 0, u, :]
+                    nc.tensor.transpose(dst, words[:, 256 * a + u : 256 * (a + 1) : 2], ident[:])
+            grp = work.tile([P, A, P, 4], BF16, name="d_grp", align_bytes=64)
+            d_bank[i] = (bank_a, bank_b)
+            d_grp[i] = grp
+
+        def s_delta(i):
+            nc.scalar.copy(
+                out=d_grp[i][:, 0:2].rearrange("p a m t -> p a (m t)").bitcast(F32).rearrange("p a (m u) -> p a m u", u=2),
+                in_=d_bank[i][0][:].rearrange("p a u m -> p a m u"),
+            )
+
+        def v_delta(i):
+            grp = d_grp[i]
+            nc.vector.tensor_copy(
+                out=grp[:, 2:3].rearrange("p a m t -> p a (m t)").bitcast(F32).rearrange("p a (m u) -> p a m u", u=2),
+                in_=d_bank[i][1][:].rearrange("p a u m -> p a m u"),
+            )
+            nc.vector.quantize_mx(
+                out=d_codes[i][:, 0:2].rearrange("p a m -> p (a m)").bitcast(E4),
+                scales=d_sc[i][:, 0:2].rearrange("p a m -> p (a m)"),
+                in_=grp[:, 0:2].rearrange("p a m t -> p (a m t)"),
+            )
+            nc.vector.quantize_mx(
+                out=d_codes[i][:, 2].bitcast(E4), scales=d_sc[i][:, 2], in_=grp[:, 2].rearrange("p m t -> p (m t)")
+            )
+
+        def mx1(c, i):
+            acc = psum.tile([P, SC], F32, name="unit_ps", bufs=2)
+            for a in range(A):
+                nc.tensor.matmul_mx(
+                    out=acc[:],
+                    lhsT=d_codes[i][:, a, :].bitcast(E4),
+                    lhsT_scale=d_sc[i][:, a, :],
+                    rhs=gw[c][:, a, :].bitcast(E5),
+                    rhs_scale=gs[:, a, SC * c : SC * (c + 1)],
+                    start=(a == 0),
+                    stop=(a == A - 1),
+                )
+            g, t = i // 4, i % 4
+            if t == 0:
+                units[(c, g)] = work.tile([P, 4, SC], F32, name="unit")
+            nc.scalar.activation(
+                out=units[(c, g)][:, t, :], in_=acc[:], func=ACT.Identity, bias=ca[:, g, t : t + 1], scale=1.0
+            )
+
+        def t_stress(c, g, tag, bufs):
+            banks = []
+            for h in range(2):
+                bank = psum.tile([P, 2, 2, P], F32, name=tag, bufs=bufs)
+                for jj in range(2):
+                    words = st[c][:, 2 * h + jj, :].bitcast(F32)
+                    for u in range(2):
+                        nc.tensor.transpose(bank[:, u, jj, :], words[:, 256 * g + u : 256 * (g + 1) : 2], ident[:])
+                banks.append(bank)
+            stress_t[(c, g)] = banks
+            pnl[(c, g)] = work.tile([P, SC, 4], BF16, name="pnl", align_bytes=64)
+            pnl_codes[(c, g)] = work.tile([P, SC], U32, name="pnl_codes", align_bytes=64, bufs=4)
+            pnl_sc[(c, g)] = work.tile([P, SC], U8, name="pnl_sc", align_bytes=64, bufs=4)
+
+        def v_mul(c, g, h):
+            cols = slice(256 * h, 256 * (h + 1))
+            bank = stress_t[(c, g)][h]
+            nc.vector.tensor_tensor(
+                out=pnl[(c, g)][:, cols, :].rearrange("p s (u e) -> p s u e", u=2),
+                in0=units[(c, g)][:, :, cols].rearrange("p (u e) s -> p s u e", u=2),
+                in1=bank[:].rearrange("p u j s -> p u (j s)").bitcast(BF16).rearrange("p u (s e) -> p s u e", e=2),
+                op=ALU.mult,
+            )
+
+        def v_quant(c, g, h):
+            cols = slice(256 * h, 256 * (h + 1))
+            nc.vector.quantize_mx(
+                out=pnl_codes[(c, g)][:, cols].bitcast(E5),
+                scales=pnl_sc[(c, g)][:, cols],
+                in_=pnl[(c, g)][:, cols, :].rearrange("p s t -> p (s t)"),
+            )
+
+        def mx2(c, j):
+            acc = psum.tile([P, B], F32, name="out_ps", bufs=2)
+            cols = slice(P * j, P * (j + 1))
+            for g in range(G):
+                nc.tensor.matmul_mx(
+                    out=acc[:],
+                    lhsT=pnl_codes[(c, g)][:, cols].bitcast(E5),
+                    lhsT_scale=pnl_sc[(c, g)][:, cols],
+                    rhs=h_codes[:, g, :].bitcast(E4),
+                    rhs_scale=h_sc[:, g, :],
+                    start=(g == 0),
+                    stop=(g == G - 1),
+                )
+            return (c, j, acc)
+
+        def v_out(item):
+            c, j, acc = item
+            res = work.tile([P, B], F32, name="res", bufs=4)
+            nc.vector.tensor_tensor(out=res[:], in0=acc[:], in1=hg[c][:, j, :], op=ALU.add)
+            s0 = SC * c + P * j
+            nc.sync.dma_start(out=out[s0 : s0 + P, :], in_=res[:])
+
+        def v_hold(g):
+            nc.vector.tensor_copy(out=h_grp[:, g], in_=h_raw[:, g].rearrange("p j w -> p w j"))
+
+        def v_hold_q(g):
+            nc.vector.quantize_mx(
+                out=h_codes[:, g].bitcast(E4), scales=h_sc[:, g], in_=h_grp[:, g].rearrange("p w j -> p (w j)")
+            )
+
+        with tc.manual_schedule():
+            nc.vector.memset(gs[:].rearrange("p a n -> p (a n)").bitcast(I32), 0)
+            warm = keep.tile([P, 1], F32, name="warm")
+            nc.vector.memset(warm[:], 0.0)
+            nc.scalar.activation(out=warm[:], in_=warm[:], func=ACT.Identity, scale=1.0)
+            load_d(0)
+            load_d(1)
+            for q in range(4):
+                nc.scalar.dma_start(
+                    out=gs[32 * q : 32 * q + 4].bitcast(I32), in_=gs_view[:, 4 * q : 4 * q + 4, :].rearrange("a r n -> r a n")
+                )
+            load_g(0)
+            nc.sync.dma_start(out=ca_raw[:], in_=carry.rearrange("(g p t) -> p g t", g=G, t=4))
+            for i in (2, 3, 4):
+                load_d(i)
+            load_st(0)
+            for i in (5, 6, 7):
+                load_d(i)
+            nc.sync.dma_start(out=h_raw[:], in_=hold.rearrange("(g p j) w -> p g j w", g=G, j=4))
+            load_g(1)
+            load_st(1)
+            load_hg(0)
+            load_g(2)
+            load_st(2)
+            load_hg(1)
+            load_g(3)
+            load_st(3)
+            load_hg(2)
+            load_hg(3)
+
+            def t_d(i):
+                t_delta(i)
+                s_delta(i)
+                v_delta(i)
+
+            t_d(0)
+            nc.vector.tensor_copy(out=ca[:], in_=ca_raw[:])
+            t_d(1)
+            mx1(0, 0)
+            t_d(2)
+            mx1(0, 1)
+            t_d(3)
+            mx1(0, 2)
+            t_d(4)
+            mx1(0, 3)
+            t_stress(0, 0, "out_ps", 2)
+            v_mul(0, 0, 0)
+            t_d(5)
+            mx1(0, 4)
+            v_mul(0, 0, 1)
+            t_d(6)
+            mx1(0, 5)
+            v_quant(0, 0, 0)
+            v_quant(0, 0, 1)
+            t_d(7)
+            mx1(0, 6)
+            v_hold(0)
+            v_hold(1)
+            mx1(0, 7)
+            v_hold_q(0)
+            v_hold_q(1)
+            t_stress(0, 1, "tr", 4)
+
+            prev = (0, 1)
+            ready = []
+            todo = []
+            for c in range(1, C):
+                for g in range(G):
+                    for t in range(4):
+                        mx1(c, 4 * g + t)
+                    v_mul(prev[0], prev[1], 0)
+                    v_mul(prev[0], prev[1], 1)
+                    v_quant(prev[0], prev[1], 0)
+                    if ready:
+                        v_out(ready.pop(0))
+                    v_quant(prev[0], prev[1], 1)
+                    if ready:
+                        v_out(ready.pop(0))
+                    if prev[1] == 1:
+                        todo = [(prev[0], j) for j in range(J)]
+                    t_stress(c, g, "tr", 4)
+                    for k in range(2):
+                        cc, j = todo.pop(0)
+                        ready.append(mx2(cc, j))
+                    prev = (c, g)
+            v_mul(prev[0], prev[1], 0)
+            v_out(ready.pop(0))
+            v_quant(prev[0], prev[1], 0)
+            v_mul(prev[0], prev[1], 1)
+            v_out(ready.pop(0))
+            v_quant(prev[0], prev[1], 1)
+            for j in range(J):
+                v_out(mx2(prev[0], j))

@@ -44,12 +44,14 @@ def tile_scenario_book_pnl_e3_kernel(tc, g_words, g_scales, delta, carry, stress
             gw.append(keep.tile([P, A, SC], U32, name="gw%d" % c, align_bytes=64))
             st.append(keep.tile([P, J, I], BF16, name="st%d" % c))
             hg.append(keep.tile([P, J, B], BF16, name="hg%d" % c))
-        gs = keep.tile([P, A, S], U8, name="gs", align_bytes=64)
+        gs = []
+        for c in range(C):
+            gs.append(keep.tile([P, A, SC], U8, name="gs%d" % c, align_bytes=64))
         h_raw = keep.tile([P, G, 4, B], BF16, name="h_raw")
         h_grp = keep.tile([P, G, B, 4], BF16, name="h_grp", align_bytes=64)
         h_codes = keep.tile([P, G, B], U32, name="h_codes", align_bytes=64)
         h_sc = keep.tile([P, G, B], U8, name="h_sc", align_bytes=64)
-        ca_raw = keep.tile([P, G, 4], BF16, name="ca_raw")
+        ca_raw = keep.tile([P, 512], BF16, name="ca_raw")
         ca = keep.tile([P, G, 4], F32, name="ca")
         d_codes = []
         d_sc = []
@@ -59,12 +61,13 @@ def tile_scenario_book_pnl_e3_kernel(tc, g_words, g_scales, delta, carry, stress
 
         d_view = delta.rearrange("(g m t) k -> g t m k", g=G, t=4)
         gw_view = g_words.rearrange("g p n t -> p g (n t)")
-        gs_view = g_scales.bitcast(I32)
+        gs_view = g_scales.bitcast(I32).rearrange("a r n -> r a n")
         st_view = stress.rearrange("(c j p) i -> c p j i", c=C, p=P)
         hg_view = hedge.rearrange("(c j p) b -> c p j b", c=C, p=P)
 
         units = {}
         stress_t = {}
+        st_re = {}
         pnl = {}
         pnl_codes = {}
         pnl_sc = {}
@@ -82,6 +85,25 @@ def tile_scenario_book_pnl_e3_kernel(tc, g_words, g_scales, delta, carry, stress
 
         def load_hg(c):
             nc.sync.dma_start(out=hg[c][:], in_=hg_view[c])
+
+        def load_gs(c):
+            for q in range(4):
+                nc.sync.dma_start(
+                    out=gs[c][32 * q : 32 * q + 4].bitcast(I32), in_=gs_view[4 * q : 4 * q + 4, :, P * c : P * (c + 1)]
+                )
+
+        def zero_gs(c):
+            nc.vector.memset(gs[c][:].rearrange("p a n -> p (a n)").bitcast(I32), 0)
+
+        def t_carry():
+            bank = psum.tile([P, 2, P], F32, name="out_ps", bufs=2)
+            words = ca_raw[:].bitcast(F32)
+            for u in range(2):
+                nc.tensor.transpose(bank[:, u, :], words[:, u : 256 : 2], ident[:])
+            nc.vector.tensor_copy(
+                out=ca[:].rearrange("p g (u e) -> p g u e", u=2),
+                in_=bank[:, :, 0:G].bitcast(BF16).rearrange("p u (g e) -> p g u e", e=2),
+            )
 
         def t_delta(i):
             bank_a = psum.tile([P, 2, 2, P], F32, name="tr", bufs=4)
@@ -124,7 +146,7 @@ def tile_scenario_book_pnl_e3_kernel(tc, g_words, g_scales, delta, carry, stress
                     lhsT=d_codes[i][:, a, :].bitcast(E4),
                     lhsT_scale=d_sc[i][:, a, :],
                     rhs=gw[c][:, a, :].bitcast(E5),
-                    rhs_scale=gs[:, a, SC * c : SC * (c + 1)],
+                    rhs_scale=gs[c][:, a, :],
                     start=(a == 0),
                     stop=(a == A - 1),
                 )
@@ -135,27 +157,37 @@ def tile_scenario_book_pnl_e3_kernel(tc, g_words, g_scales, delta, carry, stress
                 out=units[(c, g)][:, t, :], in_=acc[:], func=ACT.Identity, bias=ca[:, g, t : t + 1], scale=1.0
             )
 
+        def reorder(c, g):
+            if g == 0:
+                st_re[c] = work.tile([P, G, J, 2, P], F32, name="st_re", bufs=2)
+            nc.scalar.copy(
+                out=st_re[c][:, g],
+                in_=st[c][:].bitcast(F32).rearrange("p j (g m u) -> p g j u m", g=G, u=2)[:, g],
+            )
+
         def t_stress(c, g, tag, bufs):
             banks = []
             for h in range(2):
                 bank = psum.tile([P, 2, 2, P], F32, name=tag, bufs=bufs)
                 for jj in range(2):
-                    words = st[c][:, 2 * h + jj, :].bitcast(F32)
                     for u in range(2):
-                        nc.tensor.transpose(bank[:, u, jj, :], words[:, 256 * g + u : 256 * (g + 1) : 2], ident[:])
+                        nc.tensor.transpose(bank[:, u, jj, :], st_re[c][:, g, 2 * h + jj, u, :], ident[:])
                 banks.append(bank)
             stress_t[(c, g)] = banks
             pnl[(c, g)] = work.tile([P, SC, 4], BF16, name="pnl", align_bytes=64)
             pnl_codes[(c, g)] = work.tile([P, SC], U32, name="pnl_codes", align_bytes=64, bufs=4)
             pnl_sc[(c, g)] = work.tile([P, SC], U8, name="pnl_sc", align_bytes=64, bufs=4)
 
-        def v_mul(c, g, h):
-            cols = slice(256 * h, 256 * (h + 1))
+        def v_mul(c, g, lo, hi):
+            h = lo // 256
+            cols = slice(lo, hi)
             bank = stress_t[(c, g)][h]
             nc.vector.tensor_tensor(
                 out=pnl[(c, g)][:, cols, :].rearrange("p s (u e) -> p s u e", u=2),
                 in0=units[(c, g)][:, :, cols].rearrange("p (u e) s -> p s u e", u=2),
-                in1=bank[:].rearrange("p u j s -> p u (j s)").bitcast(BF16).rearrange("p u (s e) -> p s u e", e=2),
+                in1=bank[:].rearrange("p u j s -> p u (j s)")[:, :, lo - 256 * h : hi - 256 * h]
+                .bitcast(BF16)
+                .rearrange("p u (s e) -> p s u e", e=2),
                 op=ALU.mult,
             )
 
@@ -167,19 +199,22 @@ def tile_scenario_book_pnl_e3_kernel(tc, g_words, g_scales, delta, carry, stress
                 in_=pnl[(c, g)][:, cols, :].rearrange("p s t -> p (s t)"),
             )
 
+        def mx2_pass(c, j, g, acc):
+            cols = slice(P * j, P * (j + 1))
+            nc.tensor.matmul_mx(
+                out=acc[:],
+                lhsT=pnl_codes[(c, g)][:, cols].bitcast(E5),
+                lhsT_scale=pnl_sc[(c, g)][:, cols],
+                rhs=h_codes[:, g, :].bitcast(E4),
+                rhs_scale=h_sc[:, g, :],
+                start=(g == 0),
+                stop=(g == G - 1),
+            )
+
         def mx2(c, j):
             acc = psum.tile([P, B], F32, name="out_ps", bufs=2)
-            cols = slice(P * j, P * (j + 1))
             for g in range(G):
-                nc.tensor.matmul_mx(
-                    out=acc[:],
-                    lhsT=pnl_codes[(c, g)][:, cols].bitcast(E5),
-                    lhsT_scale=pnl_sc[(c, g)][:, cols],
-                    rhs=h_codes[:, g, :].bitcast(E4),
-                    rhs_scale=h_sc[:, g, :],
-                    start=(g == 0),
-                    stop=(g == G - 1),
-                )
+                mx2_pass(c, j, g, acc)
             return (c, j, acc)
 
         def v_out(item):
@@ -198,30 +233,32 @@ def tile_scenario_book_pnl_e3_kernel(tc, g_words, g_scales, delta, carry, stress
             )
 
         with tc.manual_schedule():
-            nc.vector.memset(gs[:].rearrange("p a n -> p (a n)").bitcast(I32), 0)
+            nc.vector.memset(ca_raw[:].bitcast(I32), 0)
+            for c in range(C):
+                zero_gs(c)
             warm = keep.tile([P, 1], F32, name="warm")
             nc.vector.memset(warm[:], 0.0)
             nc.scalar.activation(out=warm[:], in_=warm[:], func=ACT.Identity, scale=1.0)
             load_d(0)
+            nc.sync.dma_start(out=ca_raw[0:G, :], in_=carry.rearrange("(g k) -> g k", g=G))
+            load_gs(0)
             load_d(1)
-            for q in range(4):
-                nc.scalar.dma_start(
-                    out=gs[32 * q : 32 * q + 4].bitcast(I32), in_=gs_view[:, 4 * q : 4 * q + 4, :].rearrange("a r n -> r a n")
-                )
             load_g(0)
-            nc.sync.dma_start(out=ca_raw[:], in_=carry.rearrange("(g p t) -> p g t", g=G, t=4))
             for i in (2, 3, 4):
                 load_d(i)
             load_st(0)
             for i in (5, 6, 7):
                 load_d(i)
-            nc.sync.dma_start(out=h_raw[:], in_=hold.rearrange("(g p j) w -> p g j w", g=G, j=4))
+            load_gs(1)
             load_g(1)
             load_st(1)
+            nc.sync.dma_start(out=h_raw[:], in_=hold.rearrange("(g p j) w -> p g j w", g=G, j=4))
             load_hg(0)
+            load_gs(2)
             load_g(2)
             load_st(2)
             load_hg(1)
+            load_gs(3)
             load_g(3)
             load_st(3)
             load_hg(2)
@@ -233,7 +270,7 @@ def tile_scenario_book_pnl_e3_kernel(tc, g_words, g_scales, delta, carry, stress
                 v_delta(i)
 
             t_d(0)
-            nc.vector.tensor_copy(out=ca[:], in_=ca_raw[:])
+            t_carry()
             t_d(1)
             mx1(0, 0)
             t_d(2)
@@ -242,51 +279,80 @@ def tile_scenario_book_pnl_e3_kernel(tc, g_words, g_scales, delta, carry, stress
             mx1(0, 2)
             t_d(4)
             mx1(0, 3)
+            reorder(0, 0)
             t_stress(0, 0, "out_ps", 2)
-            v_mul(0, 0, 0)
+            v_mul(0, 0, 0, 256)
             t_d(5)
             mx1(0, 4)
-            v_mul(0, 0, 1)
+            v_mul(0, 0, 256, 512)
             t_d(6)
             mx1(0, 5)
             v_quant(0, 0, 0)
             v_quant(0, 0, 1)
             t_d(7)
             mx1(0, 6)
-            v_hold(0)
-            v_hold(1)
+            reorder(0, 1)
             mx1(0, 7)
-            v_hold_q(0)
-            v_hold_q(1)
             t_stress(0, 1, "tr", 4)
+            reorder(1, 0)
 
-            prev = (0, 1)
-            ready = []
-            todo = []
             for c in range(1, C):
-                for g in range(G):
-                    for t in range(4):
-                        mx1(c, 4 * g + t)
-                    v_mul(prev[0], prev[1], 0)
-                    v_mul(prev[0], prev[1], 1)
-                    v_quant(prev[0], prev[1], 0)
-                    if ready:
-                        v_out(ready.pop(0))
-                    v_quant(prev[0], prev[1], 1)
-                    if ready:
-                        v_out(ready.pop(0))
-                    if prev[1] == 1:
-                        todo = [(prev[0], j) for j in range(J)]
-                    t_stress(c, g, "tr", 4)
-                    for k in range(2):
-                        cc, j = todo.pop(0)
-                        ready.append(mx2(cc, j))
-                    prev = (c, g)
-            v_mul(prev[0], prev[1], 0)
-            v_out(ready.pop(0))
-            v_quant(prev[0], prev[1], 0)
-            v_mul(prev[0], prev[1], 1)
-            v_out(ready.pop(0))
-            v_quant(prev[0], prev[1], 1)
+                for i in range(4):
+                    mx1(c, i)
+                    if i == 1:
+                        reorder(c, 1)
+                v_mul(c - 1, 1, 0, 256)
+                v_mul(c - 1, 1, 256, 512)
+                v_quant(c - 1, 1, 0)
+                if c == 1:
+                    v_hold(0)
+                    v_quant(c - 1, 1, 1)
+                    v_hold(1)
+                    v_hold_q(0)
+                    v_hold_q(1)
+                else:
+                    v_quant(c - 1, 1, 1)
+                t_stress(c, 0, "tr", 4)
+                t_stress(c, 1, "tr", 4)
+                outs = []
+                if c > 1:
+                    outs.append(mx2(c - 1, 0))
+                    outs.append(mx2(c - 1, 1))
+                for i in range(4, 8):
+                    mx1(c, i)
+                    if c > 1 and i in (5, 6):
+                        outs.append(mx2(c - 1, i - 3))
+                if c == 1:
+                    outs = [mx2(c - 1, j) for j in range(J)]
+                if c + 1 < C:
+                    reorder(c + 1, 0)
+                v_mul(c, 0, 0, 256)
+                if c > 1:
+                    v_out(outs.pop(0))
+                v_mul(c, 0, 256, 512)
+                if c > 1:
+                    v_out(outs.pop(0))
+                v_quant(c, 0, 0)
+                v_out(outs.pop(0))
+                v_quant(c, 0, 1)
+                while outs:
+                    v_out(outs.pop(0))
+            c = C - 1
+            accs = []
             for j in range(J):
-                v_out(mx2(prev[0], j))
+                if j < 2:
+                    acc = psum.tile([P, B], F32, name="out_ps", bufs=2)
+                else:
+                    acc = psum.tile([P, B], F32, name="tr", bufs=4)
+                mx2_pass(c, j, 0, acc)
+                accs.append((c, j, acc))
+            v_mul(c, 1, 0, 128)
+            v_mul(c, 1, 128, 256)
+            v_mul(c, 1, 256, 384)
+            v_quant(c, 1, 0)
+            v_mul(c, 1, 384, 512)
+            for j in range(J):
+                mx2_pass(c, j, 1, accs[j][2])
+                if j == 1:
+                    v_quant(c, 1, 1)
+                v_out(accs[j])

@@ -157,12 +157,12 @@ def tile_scenario_book_pnl_e3_kernel(tc, g_words, g_scales, delta, carry, stress
                 out=units[(c, g)][:, t, :], in_=acc[:], func=ACT.Identity, bias=ca[:, g, t : t + 1], scale=1.0
             )
 
-        def reorder(c, g):
-            if g == 0:
+        def reorder(c, g, h):
+            if g == 0 and h == 0:
                 st_re[c] = work.tile([P, G, J, 2, P], F32, name="st_re", bufs=2)
             nc.scalar.copy(
-                out=st_re[c][:, g],
-                in_=st[c][:].bitcast(F32).rearrange("p j (g m u) -> p g j u m", g=G, u=2)[:, g],
+                out=st_re[c][:, g, 2 * h : 2 * h + 2],
+                in_=st[c][:].bitcast(F32).rearrange("p j (g m u) -> p g j u m", g=G, u=2)[:, g, 2 * h : 2 * h + 2],
             )
 
         def t_stress(c, g, tag, bufs):
@@ -171,10 +171,14 @@ def tile_scenario_book_pnl_e3_kernel(tc, g_words, g_scales, delta, carry, stress
                 bank = psum.tile([P, 2, 2, P], F32, name=tag, bufs=bufs)
                 for jj in range(2):
                     for u in range(2):
-                        nc.tensor.transpose(bank[:, u, jj, :], st_re[c][:, g, 2 * h + jj, u, :], ident[:])
+                        if c == 0:
+                            words = st[c][:, 2 * h + jj, :].bitcast(F32)[:, 256 * g + u : 256 * (g + 1) : 2]
+                        else:
+                            words = st_re[c][:, g, 2 * h + jj, u, :]
+                        nc.tensor.transpose(bank[:, u, jj, :], words, ident[:])
                 banks.append(bank)
             stress_t[(c, g)] = banks
-            pnl[(c, g)] = work.tile([P, SC, 4], BF16, name="pnl", align_bytes=64)
+            pnl[(c, g)] = work.tile([P, SC, 4], BF16, name="pnl", align_bytes=64, bufs=2)
             pnl_codes[(c, g)] = work.tile([P, SC], U32, name="pnl_codes", align_bytes=64, bufs=4)
             pnl_sc[(c, g)] = work.tile([P, SC], U8, name="pnl_sc", align_bytes=64, bufs=4)
 
@@ -219,10 +223,31 @@ def tile_scenario_book_pnl_e3_kernel(tc, g_words, g_scales, delta, carry, stress
 
         def v_out(item):
             c, j, acc = item
-            res = work.tile([P, B], F32, name="res", bufs=4)
+            res = work.tile([P, B], F32, name="res", bufs=5)
             nc.vector.tensor_tensor(out=res[:], in0=acc[:], in1=hg[c][:, j, :], op=ALU.add)
             s0 = SC * c + P * j
             nc.sync.dma_start(out=out[s0 : s0 + P, :], in_=res[:])
+
+        def store(c, j, res):
+            s0 = SC * c + P * j
+            nc.sync.dma_start(out=out[s0 : s0 + P, :], in_=res[:])
+
+        def s_evac(item):
+            raw = work.tile([P, B], F32, name="res_raw", bufs=4)
+            nc.scalar.copy(out=raw[:], in_=item[2][:])
+            return raw
+
+        def v_add(item, raw):
+            res = work.tile([P, B], F32, name="res", bufs=5)
+            nc.vector.tensor_tensor(out=res[:], in0=raw[:], in1=hg[item[0]][:, item[1], :], op=ALU.add)
+            store(item[0], item[1], res)
+
+        def g_add(item, raw):
+            res = work.tile([P, B], F32, name="res_g", bufs=4)
+            for k in range(0, B, 256):
+                cols = slice(k, k + 256)
+                nc.gpsimd.tensor_tensor(out=res[:, cols], in0=raw[:, cols], in1=hg[item[0]][:, item[1], cols], op=ALU.add)
+            return (item[0], item[1], res)
 
         def v_hold(g):
             nc.vector.tensor_copy(out=h_grp[:, g], in_=h_raw[:, g].rearrange("p j w -> p w j"))
@@ -244,11 +269,9 @@ def tile_scenario_book_pnl_e3_kernel(tc, g_words, g_scales, delta, carry, stress
             load_gs(0)
             load_d(1)
             load_g(0)
-            for i in (2, 3, 4):
+            for i in range(2, 8):
                 load_d(i)
             load_st(0)
-            for i in (5, 6, 7):
-                load_d(i)
             load_gs(1)
             load_g(1)
             load_st(1)
@@ -270,44 +293,45 @@ def tile_scenario_book_pnl_e3_kernel(tc, g_words, g_scales, delta, carry, stress
                 v_delta(i)
 
             t_d(0)
-            t_carry()
             t_d(1)
+            t_carry()
             mx1(0, 0)
             t_d(2)
-            mx1(0, 1)
             t_d(3)
+            mx1(0, 1)
             mx1(0, 2)
             t_d(4)
-            mx1(0, 3)
-            reorder(0, 0)
-            t_stress(0, 0, "out_ps", 2)
-            v_mul(0, 0, 0, 256)
             t_d(5)
+            mx1(0, 3)
+            t_stress(0, 0, "out_ps", 2)
             mx1(0, 4)
-            v_mul(0, 0, 256, 512)
+            v_mul(0, 0, 0, 256)
             t_d(6)
+            v_mul(0, 0, 256, 512)
             mx1(0, 5)
+            t_d(7)
             v_quant(0, 0, 0)
             v_quant(0, 0, 1)
-            t_d(7)
             mx1(0, 6)
-            reorder(0, 1)
+            reorder(1, 0, 0)
+            v_hold(0)
+            reorder(1, 0, 1)
             mx1(0, 7)
+            reorder(1, 1, 0)
             t_stress(0, 1, "tr", 4)
-            reorder(1, 0)
+            reorder(1, 1, 1)
 
             for c in range(1, C):
                 for i in range(4):
                     mx1(c, i)
-                    if i == 1:
-                        reorder(c, 1)
+                    if c + 1 < C and i in (1, 3):
+                        reorder(c + 1, 0, i // 2)
                 v_mul(c - 1, 1, 0, 256)
                 v_mul(c - 1, 1, 256, 512)
                 v_quant(c - 1, 1, 0)
                 if c == 1:
-                    v_hold(0)
-                    v_quant(c - 1, 1, 1)
                     v_hold(1)
+                    v_quant(c - 1, 1, 1)
                     v_hold_q(0)
                     v_hold_q(1)
                 else:
@@ -315,44 +339,55 @@ def tile_scenario_book_pnl_e3_kernel(tc, g_words, g_scales, delta, carry, stress
                 t_stress(c, 0, "tr", 4)
                 t_stress(c, 1, "tr", 4)
                 outs = []
-                if c > 1:
+                if c == 2:
                     outs.append(mx2(c - 1, 0))
                     outs.append(mx2(c - 1, 1))
                 for i in range(4, 8):
                     mx1(c, i)
-                    if c > 1 and i in (5, 6):
+                    if c == 2 and i in (5, 6):
                         outs.append(mx2(c - 1, i - 3))
+                    if c + 1 < C and i in (5, 7):
+                        reorder(c + 1, 1, (i - 5) // 2)
                 if c == 1:
                     outs = [mx2(c - 1, j) for j in range(J)]
-                if c + 1 < C:
-                    reorder(c + 1, 0)
                 v_mul(c, 0, 0, 256)
-                if c > 1:
+                if c == 2:
                     v_out(outs.pop(0))
                 v_mul(c, 0, 256, 512)
-                if c > 1:
+                if c == 2:
                     v_out(outs.pop(0))
                 v_quant(c, 0, 0)
-                v_out(outs.pop(0))
+                if c < 3:
+                    v_out(outs.pop(0))
                 v_quant(c, 0, 1)
                 while outs:
                     v_out(outs.pop(0))
             c = C - 1
+            held = []
+            for j in range(J):
+                item = mx2(c - 1, j)
+                held.append(g_add(item, s_evac(item)))
             accs = []
             for j in range(J):
                 if j < 2:
                     acc = psum.tile([P, B], F32, name="out_ps", bufs=2)
                 else:
                     acc = psum.tile([P, B], F32, name="tr", bufs=4)
-                mx2_pass(c, j, 0, acc)
                 accs.append((c, j, acc))
+            for j in (2, 3, 0, 1):
+                mx2_pass(c, j, 0, accs[j][2])
             v_mul(c, 1, 0, 128)
             v_mul(c, 1, 128, 256)
             v_mul(c, 1, 256, 384)
             v_quant(c, 1, 0)
             v_mul(c, 1, 384, 512)
+            store(*held[0])
+            store(*held[1])
+            store(*held[2])
             for j in range(J):
                 mx2_pass(c, j, 1, accs[j][2])
                 if j == 1:
                     v_quant(c, 1, 1)
                 v_out(accs[j])
+                if j == 1:
+                    store(*held[3])

from contextlib import ExitStack

import concourse.mybir as mybir
from concourse.masks import make_identity

F, S, I, B = 1536, 2048, 1024, 512
FLOPS = 2 * S * F * I + 2 * S * I * B

F32 = mybir.dt.float32
BF16 = mybir.dt.bfloat16
U32 = mybir.dt.uint32
I32 = mybir.dt.int32
U8 = mybir.dt.uint8
E4 = mybir.dt.float8_e4m3fn_x4
E5 = mybir.dt.float8_e5m2_x4
ACT = mybir.ActivationFunctionType
ALU = mybir.AluOpType

P = 128
A = F // 512
G = I // 512
SC = 512
C = S // SC
J = SC // P


def tile_scenario_book_pnl_e3_kernel(tc, g_words, g_scales, delta, carry, stress, hold, hedge, out):
    nc = tc.nc
    with ExitStack() as ctx:
        keep = ctx.enter_context(tc.tile_pool(name="keep", bufs=1))
        work = ctx.enter_context(tc.tile_pool(name="work", bufs=3))
        psum = ctx.enter_context(tc.psum_pool(name="psum", bufs=2))

        ident = keep.tile([P, P], F32, name="ident")
        make_identity(nc, ident[:])

        d_raw = []
        for i in range(8):
            d_raw.append(keep.tile([P, F], BF16, name="d_raw%d" % i))
        gw = []
        st = []
        hg = []
        for c in range(C):
            gw.append(keep.tile([P, A, SC], U32, name="gw%d" % c, align_bytes=64))
            st.append(keep.tile([P, J, I], BF16, name="st%d" % c))
            hg.append(keep.tile([P, J, B], BF16, name="hg%d" % c))
        gs = []
        for c in range(C):
            gs.append(keep.tile([P, A, SC], U8, name="gs%d" % c, align_bytes=64))
        h_raw = keep.tile([P, G, 4, B], BF16, name="h_raw")
        h_grp = keep.tile([P, G, B, 4], BF16, name="h_grp", align_bytes=64)
        h_codes = keep.tile([P, G, B], U32, name="h_codes", align_bytes=64)
        h_sc = keep.tile([P, G, B], U8, name="h_sc", align_bytes=64)
        ca_raw = keep.tile([P, 512], BF16, name="ca_raw")
        ca = keep.tile([P, G, 4], F32, name="ca")
        d_codes = []
        d_sc = []
        for i in range(8):
            d_codes.append(keep.tile([P, A, P], U32, name="d_codes%d" % i, align_bytes=64))
            d_sc.append(keep.tile([P, A, P], U8, name="d_sc%d" % i, align_bytes=64))

        d_view = delta.rearrange("(g m t) k -> g t m k", g=G, t=4)
        gw_view = g_words.rearrange("g p n t -> p g (n t)")
        gs_view = g_scales.bitcast(I32).rearrange("a r n -> r a n")
        st_view = stress.rearrange("(c j p) i -> c p j i", c=C, p=P)
        hg_view = hedge.rearrange("(c j p) b -> c p j b", c=C, p=P)

        units = {}
        stress_t = {}
        st_re = {}
        pnl = {}
        pnl_codes = {}
        pnl_sc = {}
        d_bank = {}
        d_grp = {}

        def load_d(i):
            nc.sync.dma_start(out=d_raw[i][:], in_=d_view[i // 4, i % 4])

        def load_g(c):
            nc.sync.dma_start(out=gw[c][:].bitcast(I32), in_=gw_view[:, :, 2048 * c : 2048 * (c + 1)].bitcast(I32))

        def load_st(c):
            nc.sync.dma_start(out=st[c][:], in_=st_view[c])

        def load_hg(c):
            nc.sync.dma_start(out=hg[c][:], in_=hg_view[c])

        def load_gs(c):
            for q in range(4):
                nc.sync.dma_start(
                    out=gs[c][32 * q : 32 * q + 4].bitcast(I32), in_=gs_view[4 * q : 4 * q + 4, :, P * c : P * (c + 1)]
                )

        def zero_gs(c):
            nc.vector.memset(gs[c][:].rearrange("p a n -> p (a n)").bitcast(I32), 0)

        def t_carry():
            bank = psum.tile([P, 2, P], F32, name="out_ps", bufs=2)
            words = ca_raw[:].bitcast(F32)
            for u in range(2):
                nc.tensor.transpose(bank[:, u, :], words[:, u : 256 : 2], ident[:])
            nc.vector.tensor_copy(
                out=ca[:].rearrange("p g (u e) -> p g u e", u=2),
                in_=bank[:, :, 0:G].bitcast(BF16).rearrange("p u (g e) -> p g u e", e=2),
            )

        def t_delta(i):
            bank_a = psum.tile([P, 2, 2, P], F32, name="tr", bufs=4)
            bank_b = psum.tile([P, 1, 2, P], F32, name="tr", bufs=4)
            words = d_raw[i][:].bitcast(F32)
            for a in range(A):
                for u in range(2):
                    dst = bank_a[:, a, u, :] if a < 2 else bank_b[:, 0, u, :]
                    nc.tensor.transpose(dst, words[:, 256 * a + u : 256 * (a + 1) : 2], ident[:])
            grp = work.tile([P, A, P, 4], BF16, name="d_grp", align_bytes=64)
            d_bank[i] = (bank_a, bank_b)
            d_grp[i] = grp

        def s_delta(i):
            nc.scalar.copy(
                out=d_grp[i][:, 0:2].rearrange("p a m t -> p a (m t)").bitcast(F32).rearrange("p a (m u) -> p a m u", u=2),
                in_=d_bank[i][0][:].rearrange("p a u m -> p a m u"),
            )

        def v_delta(i):
            grp = d_grp[i]
            nc.vector.tensor_copy(
                out=grp[:, 2:3].rearrange("p a m t -> p a (m t)").bitcast(F32).rearrange("p a (m u) -> p a m u", u=2),
                in_=d_bank[i][1][:].rearrange("p a u m -> p a m u"),
            )
            nc.vector.quantize_mx(
                out=d_codes[i][:, 0:2].rearrange("p a m -> p (a m)").bitcast(E4),
                scales=d_sc[i][:, 0:2].rearrange("p a m -> p (a m)"),
                in_=grp[:, 0:2].rearrange("p a m t -> p (a m t)"),
            )
            nc.vector.quantize_mx(
                out=d_codes[i][:, 2].bitcast(E4), scales=d_sc[i][:, 2], in_=grp[:, 2].rearrange("p m t -> p (m t)")
            )

        def mx1(c, i):
            acc = psum.tile([P, SC], F32, name="unit_ps", bufs=2)
            for a in range(A):
                nc.tensor.matmul_mx(
                    out=acc[:],
                    lhsT=d_codes[i][:, a, :].bitcast(E4),
                    lhsT_scale=d_sc[i][:, a, :],
                    rhs=gw[c][:, a, :].bitcast(E5),
                    rhs_scale=gs[c][:, a, :],
                    start=(a == 0),
                    stop=(a == A - 1),
                )
            g, t = i // 4, i % 4
            if t == 0:
                units[(c, g)] = work.tile([P, 4, SC], F32, name="unit")
            nc.scalar.activation(
                out=units[(c, g)][:, t, :], in_=acc[:], func=ACT.Identity, bias=ca[:, g, t : t + 1], scale=1.0
            )

        def reorder(c, g, h):
            if g == 0 and h == 0:
                st_re[c] = work.tile([P, G, J, 2, P], F32, name="st_re", bufs=2)
            nc.scalar.copy(
                out=st_re[c][:, g, 2 * h : 2 * h + 2],
                in_=st[c][:].bitcast(F32).rearrange("p j (g m u) -> p g j u m", g=G, u=2)[:, g, 2 * h : 2 * h + 2],
            )

        def t_stress(c, g, tag, bufs):
            banks = []
            for h in range(2):
                bank = psum.tile([P, 2, 2, P], F32, name=tag, bufs=bufs)
                for jj in range(2):
                    for u in range(2):
                        if c == 0:
                            words = st[c][:, 2 * h + jj, :].bitcast(F32)[:, 256 * g + u : 256 * (g + 1) : 2]
                        else:
                            words = st_re[c][:, g, 2 * h + jj, u, :]
                        nc.tensor.transpose(bank[:, u, jj, :], words, ident[:])
                banks.append(bank)
            stress_t[(c, g)] = banks
            pnl[(c, g)] = work.tile([P, SC, 4], BF16, name="pnl", align_bytes=64, bufs=2)
            pnl_codes[(c, g)] = work.tile([P, SC], U32, name="pnl_codes", align_bytes=64, bufs=4)
            pnl_sc[(c, g)] = work.tile([P, SC], U8, name="pnl_sc", align_bytes=64, bufs=4)

        def v_mul(c, g, lo, hi):
            h = lo // 256
            cols = slice(lo, hi)
            bank = stress_t[(c, g)][h]
            nc.vector.tensor_tensor(
                out=pnl[(c, g)][:, cols, :].rearrange("p s (u e) -> p s u e", u=2),
                in0=units[(c, g)][:, :, cols].rearrange("p (u e) s -> p s u e", u=2),
                in1=bank[:].rearrange("p u j s -> p u (j s)")[:, :, lo - 256 * h : hi - 256 * h]
                .bitcast(BF16)
                .rearrange("p u (s e) -> p s u e", e=2),
                op=ALU.mult,
            )

        def v_quant(c, g, h):
            cols = slice(256 * h, 256 * (h + 1))
            nc.vector.quantize_mx(
                out=pnl_codes[(c, g)][:, cols].bitcast(E5),
                scales=pnl_sc[(c, g)][:, cols],
                in_=pnl[(c, g)][:, cols, :].rearrange("p s t -> p (s t)"),
            )

        def mx2_pass(c, j, g, acc):
            cols = slice(P * j, P * (j + 1))
            nc.tensor.matmul_mx(
                out=acc[:],
                lhsT=pnl_codes[(c, g)][:, cols].bitcast(E5),
                lhsT_scale=pnl_sc[(c, g)][:, cols],
                rhs=h_codes[:, g, :].bitcast(E4),
                rhs_scale=h_sc[:, g, :],
                start=(g == 0),
                stop=(g == G - 1),
            )

        def mx2(c, j):
            acc = psum.tile([P, B], F32, name="out_ps", bufs=2)
            for g in range(G):
                mx2_pass(c, j, g, acc)
            return (c, j, acc)

        def v_out(item):
            c, j, acc = item
            res = work.tile([P, B], F32, name="res", bufs=5)
            nc.vector.tensor_tensor(out=res[:], in0=acc[:], in1=hg[c][:, j, :], op=ALU.add)
            s0 = SC * c + P * j
            nc.sync.dma_start(out=out[s0 : s0 + P, :], in_=res[:])

        def store(c, j, res):
            s0 = SC * c + P * j
            nc.sync.dma_start(out=out[s0 : s0 + P, :], in_=res[:])

        def s_evac(item):
            raw = work.tile([P, B], F32, name="res_raw", bufs=4)
            nc.scalar.copy(out=raw[:], in_=item[2][:])
            return raw

        def v_add(item, raw):
            res = work.tile([P, B], F32, name="res", bufs=5)
            nc.vector.tensor_tensor(out=res[:], in0=raw[:], in1=hg[item[0]][:, item[1], :], op=ALU.add)
            store(item[0], item[1], res)

        def g_add(item, raw):
            res = work.tile([P, B], F32, name="res_g", bufs=4)
            for k in range(0, B, 256):
                cols = slice(k, k + 256)
                nc.gpsimd.tensor_tensor(out=res[:, cols], in0=raw[:, cols], in1=hg[item[0]][:, item[1], cols], op=ALU.add)
            return (item[0], item[1], res)

        def v_hold(g):
            nc.vector.tensor_copy(out=h_grp[:, g], in_=h_raw[:, g].rearrange("p j w -> p w j"))

        def v_hold_q(g):
            nc.vector.quantize_mx(
                out=h_codes[:, g].bitcast(E4), scales=h_sc[:, g], in_=h_grp[:, g].rearrange("p w j -> p (w j)")
            )

        with tc.manual_schedule():
            nc.vector.memset(ca_raw[:].bitcast(I32), 0)
            for c in range(C):
                zero_gs(c)
            warm = keep.tile([P, 1], F32, name="warm")
            nc.vector.memset(warm[:], 0.0)
            nc.scalar.activation(out=warm[:], in_=warm[:], func=ACT.Identity, scale=1.0)
            load_d(0)
            nc.sync.dma_start(out=ca_raw[0:G, :], in_=carry.rearrange("(g k) -> g k", g=G))
            load_gs(0)
            load_d(1)
            load_g(0)
            for i in range(2, 8):
                load_d(i)
            load_st(0)
            load_gs(1)
            load_g(1)
            load_st(1)
            nc.sync.dma_start(out=h_raw[:], in_=hold.rearrange("(g p j) w -> p g j w", g=G, j=4))
            load_hg(0)
            load_gs(2)
            load_g(2)
            load_st(2)
            load_hg(1)
            load_gs(3)
            load_g(3)
            load_st(3)
            load_hg(2)
            load_hg(3)

            def t_d(i):
                t_delta(i)
                s_delta(i)
                v_delta(i)

            t_d(0)
            t_d(1)
            t_carry()
            mx1(0, 0)
            t_d(2)
            t_d(3)
            mx1(0, 1)
            mx1(0, 2)
            t_d(4)
            t_d(5)
            mx1(0, 3)
            t_stress(0, 0, "out_ps", 2)
            mx1(0, 4)
            v_mul(0, 0, 0, 256)
            t_d(6)
            v_mul(0, 0, 256, 512)
            mx1(0, 5)
            t_d(7)
            v_quant(0, 0, 0)
            v_quant(0, 0, 1)
            mx1(0, 6)
            reorder(1, 0, 0)
            v_hold(0)
            reorder(1, 0, 1)
            mx1(0, 7)
            reorder(1, 1, 0)
            t_stress(0, 1, "tr", 4)
            reorder(1, 1, 1)

            for c in range(1, C):
                for i in range(4):
                    mx1(c, i)
                    if c + 1 < C and i in (1, 3):
                        reorder(c + 1, 0, i // 2)
                v_mul(c - 1, 1, 0, 256)
                v_mul(c - 1, 1, 256, 512)
                v_quant(c - 1, 1, 0)
                if c == 1:
                    v_hold(1)
                    v_quant(c - 1, 1, 1)
                    v_hold_q(0)
                    v_hold_q(1)
                else:
                    v_quant(c - 1, 1, 1)
                t_stress(c, 0, "tr", 4)
                t_stress(c, 1, "tr", 4)
                outs = []
                if c == 2:
                    outs.append(mx2(c - 1, 0))
                    outs.append(mx2(c - 1, 1))
                for i in range(4, 8):
                    mx1(c, i)
                    if c == 2 and i in (5, 6):
                        outs.append(mx2(c - 1, i - 3))
                    if c + 1 < C and i in (5, 7):
                        reorder(c + 1, 1, (i - 5) // 2)
                if c == 1:
                    outs = [mx2(c - 1, j) for j in range(J)]
                v_mul(c, 0, 0, 256)
                if c == 2:
                    v_out(outs.pop(0))
                v_mul(c, 0, 256, 512)
                if c == 2:
                    v_out(outs.pop(0))
                v_quant(c, 0, 0)
                if c < 3:
                    v_out(outs.pop(0))
                v_quant(c, 0, 1)
                while outs:
                    v_out(outs.pop(0))
            c = C - 1
            held = []
            for j in range(J):
                item = mx2(c - 1, j)
                held.append(g_add(item, s_evac(item)))
            accs = []
            for j in range(J):
                if j < 2:
                    acc = psum.tile([P, B], F32, name="out_ps", bufs=2)
                else:
                    acc = psum.tile([P, B], F32, name="tr", bufs=4)
                accs.append((c, j, acc))
            for j in (2, 3, 0, 1):
                mx2_pass(c, j, 0, accs[j][2])
            v_mul(c, 1, 0, 128)
            v_mul(c, 1, 128, 256)
            v_mul(c, 1, 256, 384)
            v_quant(c, 1, 0)
            v_mul(c, 1, 384, 512)
            store(*held[0])
            store(*held[1])
            store(*held[2])
            for j in range(J):
                mx2_pass(c, j, 1, accs[j][2])
                if j == 1:
                    v_quant(c, 1, 1)
                v_out(accs[j])
                if j == 1:
                    store(*held[3])
